import numpy as np
import ml_dtypes


def mxq(x, axis, fmt="e4m3"):
    dtype, down = {"e4m3": (ml_dtypes.float8_e4m3fn, 7), "e5m2": (ml_dtypes.float8_e5m2, 14)}[fmt]
    v = np.moveaxis(np.asarray(x, np.float32).astype(ml_dtypes.bfloat16).astype(np.float64), axis, -1)
    blocks = v.reshape(v.shape[:-1] + (-1, 32))
    amax = np.abs(blocks).max(-1, keepdims=True)
    byte = np.maximum(np.where(amax > 0, np.frexp(amax)[1] - 1 + 127, 0) - down, 1)
    scale = np.exp2(byte - 127.0)
    codes = (blocks / scale).astype(np.float32).astype(dtype).astype(np.float64)
    return np.moveaxis((codes * scale).reshape(v.shape), -1, axis)


WIDE = False


def mx_kscale(k):
    if not WIDE:
        return np.ones(k)
    levels = np.array([10, -10, 5, -5, 0])
    if k % 512:
        return np.exp2(np.random.permutation(np.resize(levels, k // 32))).repeat(32)
    a = np.empty((k // 512, 16))
    for p in range(k // 512):
        a[p, :8] = np.random.permutation(np.resize(levels, 8))
        for g in range(8):
            far = levels[np.abs(levels - a[p, g]) >= 10]
            a[p, g + 8] = far[np.random.randint(len(far))]
    return np.exp2(a.ravel()).repeat(32)


def f64(x):
    return np.asarray(x).astype(np.float64)


def striped(idx):
    return np.tile(idx.reshape(-1, 16).T, (8, 1)).astype(np.uint16)


def unstriped(offs):
    return offs[:16].T.reshape(-1).astype(np.int64)


E2M1 = np.array([0.0, 0.5, 1.0, 1.5, 2.0, 3.0, 4.0, 6.0, -0.0, -0.5, -1.0, -1.5, -2.0, -3.0, -4.0, -6.0])


def pack_weight(w, fmt):
    k, n = w.shape
    w = f64(np.asarray(w, np.float32).astype(ml_dtypes.bfloat16)).reshape(k // 32, 32, n)
    amax = np.abs(w).max(1)
    if fmt == "e4m3":
        byte = np.frexp(amax)[1] - 1 + 127 - 7
    else:
        mant, ex = np.frexp(amax / 6.0)
        byte = np.where(mant > 0.5, ex, ex - 1) + 127
    byte = np.clip(np.where(amax > 0, byte, 1), 1, 254)
    scaled = (w * np.exp2(127.0 - byte)[:, None, :]).reshape(k, n).astype(np.float32)
    by_word = np.ascontiguousarray(scaled.reshape(k // 512, 128, 4, n).transpose(0, 1, 3, 2))
    if fmt == "e4m3":
        words = by_word.astype(ml_dtypes.float8_e4m3fn).view(np.uint8)
    else:
        c = by_word.astype(ml_dtypes.float4_e2m1fn).view(np.uint8) & 0xF
        words = (c[..., 0::2] | (c[..., 1::2] << 4)).reshape(k // 512, 128, 2 * n)
    return np.ascontiguousarray(words), np.ascontiguousarray(byte.astype(np.uint8).reshape(k // 512, 16, n))


def unpack_weight(words, scales, fmt):
    g, _, n = scales.shape
    words = np.ascontiguousarray(words).reshape(g, 128, n, -1)
    if fmt == "e4m3":
        vals = words.view(ml_dtypes.float8_e4m3fn).astype(np.float64)
    else:
        nib = np.empty((g, 128, n, 4), np.uint8)
        nib[..., 0::2] = words & 0xF
        nib[..., 1::2] = words >> 4
        vals = E2M1[nib]
    vals = vals * np.repeat(np.exp2(scales.astype(np.float64) - 127.0), 8, axis=1)[..., None]
    return vals.transpose(0, 1, 3, 2).reshape(g * 512, n)


K, T, E, C, N, TOP = 256, 768, 12, 256, 512, 4


def by_expert(wq, xq):
    return np.concatenate([wq[e].T @ xq[:, e * C:(e + 1) * C] for e in range(E)], axis=1)


def setup_inputs():
    n = np.random.standard_normal
    v = mx_kscale(N)
    deal = np.repeat(np.arange(E), C).reshape(TOP, T)[:, np.random.permutation(T)]
    deal = np.take_along_axis(deal, np.argsort(np.random.rand(TOP, T), axis=0), axis=0)
    for _ in range(8):
        s_, t_ = np.random.permutation(T).reshape(2, -1); r = np.random.randint(TOP, size=T // 2); x, y = deal[r, s_].copy(), deal[r, t_].copy()
        ok = ~((deal[:, s_] == y).any(0) | (deal[:, t_] == x).any(0)); deal[r[ok], s_[ok]] = y[ok]; deal[r[ok], t_[ok]] = x[ok]
    order = np.argsort(deal.reshape(-1) + 0.5 * np.random.rand(TOP * T))
    slot_token = order % T; pos = np.empty(TOP * T, np.int64); pos[order] = np.arange(TOP * T); pos = pos.reshape(TOP, T)
    g = np.random.uniform(0.5, 1.5, (TOP, T)); g = g / g.sum(0)
    w_slot = np.empty(E * C)
    for r in range(TOP): w_slot[pos[r]] = g[r]
    dq = pack_weight(n((N, T)) * v[:, None], "e4m3")
    dk = pack_weight(n((N, T)) * v[:, None], "e4m3")
    dv = pack_weight(n((N, T)) * v[:, None], "e4m3")
    wq = [pack_weight(m, "e4m3") for m in n((E, N, K)) / np.sqrt(N) / v[None, :, None]]
    wv = [pack_weight(m, "e2m1") for m in n((E, N, K)) / np.sqrt(N) / v[None, :, None]]
    return {
        "dq_words": dq[0],
        "dq_scales": dq[1],
        "dk_words": dk[0],
        "dk_scales": dk[1],
        "dv_words": dv[0],
        "dv_scales": dv[1],
        "wq_words": np.stack([m[0] for m in wq]),
        "wq_scales": np.stack([m[1] for m in wq]),
        "wk": (n((E, N, K)) / np.sqrt(N) / v[None, :, None]).astype(np.float32),
        "wv_words": np.stack([m[0] for m in wv]),
        "wv_scales": np.stack([m[1] for m in wv]),
        "gate": (np.tile(w_slot, (128, 1))).astype(np.float32),
        "offs": striped(slot_token),
        "pos1": striped(pos[0]),
        "pos2": striped(pos[1]),
        "pos3": striped(pos[2]),
        "pos4": striped(pos[3]),
    }


def reference(dq_words, dq_scales, dk_words, dk_scales, dv_words, dv_scales, wq_words, wq_scales, wk, wv_words, wv_scales, gate, offs, pos1, pos2, pos3, pos4):
    wq = np.stack([unpack_weight(wq_words[e], wq_scales[e], "e4m3") for e in range(E)])
    wkq = mxq(f64(wk), 1, "e4m3")
    wv = np.stack([unpack_weight(wv_words[e], wv_scales[e], "e2m1") for e in range(E)])
    idx = unstriped(offs)
    gq, gk, gv = [unpack_weight(w, s, "e4m3")[:, idx] for w, s in ((dq_words, dq_scales), (dk_words, dk_scales), (dv_words, dv_scales))]
    dx = f64(gate[:1]) * (by_expert(wq, gq) + by_expert(wkq, gk) + by_expert(wv, gv))
    out = dx[:, unstriped(pos1)] + dx[:, unstriped(pos2)] + dx[:, unstriped(pos3)] + dx[:, unstriped(pos4)]
    return out

@@ -1,0 +1,245 @@
+from contextlib import ExitStack
+
+import concourse.mybir as mybir
+from concourse.masks import make_identity
+
+K, T, E, C, N, TOP = 256, 768, 12, 256, 512, 4
+SLOTS = E * C
+FLOPS = 2 * 3 * SLOTS * N * K
+
+F32 = mybir.dt.float32
+BF16 = mybir.dt.bfloat16
+I32 = mybir.dt.int32
+U32 = mybir.dt.uint32
+U16 = mybir.dt.uint16
+U8 = mybir.dt.uint8
+FP8X4 = mybir.dt.float8_e4m3fn_x4
+FP4X4 = mybir.dt.float4_e2m1fn_x4
+MULT = mybir.AluOpType.mult
+ADD = mybir.AluOpType.add
+COPY = mybir.ActivationFunctionType.Copy
+
+P = 128
+PACK = 4
+WINDOW = 1024
+HALVES = K // P
+BLOCKS = C // P
+LAST = E - 1
+STRETCHES = [(0, 3), (3, 6), (6, 9), (9, 11), (11, 12)]
+GROUP = 3
+RAW_BYTES = GROUP * PACK * K * 4
+ACC_BANKS = 4
+
+
+def tile_moe_qkb_kernel(
+    tc, dq_words, dq_scales, dk_words, dk_scales, dv_words, dv_scales, wq_words, wq_scales, wk,
+    wv_words, wv_scales, gate, offs, pos1, pos2, pos3, pos4, out,
+):
+    nc = tc.nc
+    with ExitStack() as ctx:
+        keep = ctx.enter_context(tc.tile_pool(name="keep", bufs=1))
+        ring = ctx.enter_context(tc.tile_pool(name="ring", bufs=3))
+        shared = ctx.enter_context(tc.tile_pool(name="shared", bufs=1))
+        acc_pool = ctx.enter_context(tc.psum_pool(name="acc", bufs=1))
+        turn_pool = ctx.enter_context(tc.psum_pool(name="turn", bufs=2))
+
+        offs_sb = keep.tile([P, SLOTS // 16], U16, name="offs_sb")
+        pos_sb = [keep.tile([P, T // 16], U16, name="pos_sb%d" % r) for r in range(TOP)]
+        nc.sync.dma_start(offs_sb[:], offs)
+
+        tok_words, tok_scales, slot_words, slot_scales = {}, {}, {}, {}
+        first_of = {e: e0 for e0, e1 in STRETCHES for e in range(e0, e1)}
+        for name, words in (("q", dq_words), ("v", dv_words), ("k", dk_words)):
+            tok_words[name] = keep.tile([P, WINDOW], I32, name="tok_words_" + name, align_bytes=64)
+            nc.vector.memset(tok_words[name][:, T:WINDOW], 0)
+            nc.sync.dma_start(tok_words[name][:, 0:T], words[0].rearrange("p t d -> p (t d)").bitcast(I32))
+        for name, scales in (("v", dv_scales), ("q", dq_scales), ("k", dk_scales)):
+            tok_scales[name] = keep.tile([P, WINDOW], U8, name="tok_scales_" + name, align_bytes=64)
+            nc.vector.memset(tok_scales[name][:].bitcast(I32), 0)
+            for r in range(4):
+                nc.sync.dma_start(tok_scales[name][r:P:32, 0:T].bitcast(I32), scales[0, r:16:4, :].bitcast(I32))
+
+        ident = keep.tile([P, P], F32, name="ident")
+        make_identity(nc, ident[:])
+
+        wq_codes = keep.tile([P, E, K * PACK], U8, name="wq_codes", align_bytes=64)
+        wv_codes = keep.tile([P, E, K * 2], U8, name="wv_codes", align_bytes=64)
+        wk_codes = keep.tile([P, E, K], U32, name="wk_codes", align_bytes=64)
+        wq_plane = keep.tile([P, E, K], U8, name="wq_plane", align_bytes=64)
+        wv_plane = keep.tile([P, E, K], U8, name="wv_plane", align_bytes=64)
+        wk_plane = keep.tile([P, E, K], U8, name="wk_plane", align_bytes=64)
+        wk_raw = [shared.tile([P, GROUP, PACK, K], F32, name="wk_raw%d" % g, align_bytes=64, offset=g * RAW_BYTES)
+                  for g in range(E // GROUP)]
+        rounded = [keep.tile([P, GROUP, K * PACK], BF16, name="rounded%d" % g, align_bytes=64)
+                   for g in range(E // GROUP)]
+        nc.vector.memset(wv_plane[:].bitcast(I32), 0)
+        nc.vector.memset(wq_plane[:].bitcast(I32), 0)
+
+        def load_wk(e):
+            nc.sync.dma_start(wk_raw[e // GROUP][:, e % GROUP, :, :], wk[e].rearrange("(p j) c -> p j c", j=PACK))
+
+        def load_packed(e0, e1):
+            nc.sync.dma_start(wv_codes[:, e0:e1, :].bitcast(I32),
+                              wv_words[e0:e1].rearrange("e s p b -> p (e s) b").bitcast(I32))
+            nc.sync.dma_start(wq_codes[:, e0:e1, :].bitcast(I32),
+                              wq_words[e0:e1].rearrange("e s p c d -> p (e s) (c d)").bitcast(I32))
+
+        gate_rows = keep.tile([P, P], F32, name="gate_rows")
+        gate_cols = keep.tile([P, E * BLOCKS], F32, name="gate_cols")
+        gate_last = keep.tile([P, C], F32, name="gate_last")
+
+        for e in range(0, 3):
+            load_wk(e)
+        for plane, scales in ((wv_plane, wv_scales), (wq_plane, wq_scales)):
+            for r in range(4):
+                nc.sync.dma_start(plane[r:P:32, :, :].bitcast(I32),
+                                  scales[:, 0, r:16:4, :].rearrange("e b c -> b e c").bitcast(I32))
+        nc.sync.dma_start(gate_rows[:], gate.rearrange("r (b p) -> (r b) p", p=P)[0:P, :])
+        load_packed(0, 3)
+        for e in range(3, 6):
+            load_wk(e)
+        load_packed(3, 6)
+        for e in range(6, 12):
+            load_wk(e)
+        load_packed(6, 12)
+        nc.sync.dma_start(gate_last[:], gate[:, LAST * C : SLOTS])
+        for r, pos in enumerate((pos1, pos2, pos3, pos4)):
+            nc.sync.dma_start(pos_sb[r][:], pos)
+
+        gate_bank = turn_pool.tile([P, 4 * P], F32, name="turn")
+        nc.tensor.transpose(gate_bank[:, 0:P], gate_rows[:], ident[:])
+        nc.scalar.copy(gate_cols[:], gate_bank[:, 0 : E * BLOCKS])
+
+        dx = [keep.tile([P, SLOTS], F32, name="dx%d" % h) for h in range(HALVES)]
+
+        used = [0] * (E // GROUP)
+
+        def slot_tile(dtype, size, sort, e0, e1, after):
+            shape, name = [P, (e1 - e0) * C], "%s_%d" % (sort, e0)
+            if after is None:
+                return keep.tile(shape, dtype, name=name, align_bytes=64)
+            offset = after * RAW_BYTES + used[after]
+            used[after] += shape[1] * size
+            assert used[after] <= RAW_BYTES
+            return shared.tile(shape, dtype, name=name, align_bytes=64, offset=offset)
+
+        def gather(dst, window, e0, e1):
+            nc.vector.tensor_copy(dst[:], window.indirect(offs_sb[:, e0 * C // 16 : e1 * C // 16]))
+
+        def gather_words(name, e0, e1, after):
+            slot_words[name, e0] = slot_tile(U32, 4, "words_" + name, e0, e1, after)
+            gather(slot_words[name, e0], tok_words[name][:].bitcast(U32), e0, e1)
+
+        def gather_scales(name, e0, e1, after):
+            slot_scales[name, e0] = slot_tile(U8, 1, "scales_" + name, e0, e1, after)
+            gather(slot_scales[name, e0], tok_scales[name][:], e0, e1)
+
+        def round_weights(e):
+            g, u = divmod(e, GROUP)
+            nc.scalar.copy(rounded[g][:, u, :].rearrange("p (g i j) -> p g j i", i=4, j=PACK),
+                           wk_raw[g][:, u, :, :].rearrange("p j (g i) -> p g j i", i=4))
+
+        def quantize(e0, e1):
+            g, u = divmod(e0, GROUP)
+            nc.vector.quantize_mx(
+                out=wk_codes[:, e0:e1, :].rearrange("p e c -> p (e c)").bitcast(FP8X4),
+                scales=wk_plane[:, e0:e1, :].rearrange("p e c -> p (e c)"),
+                in_=rounded[g][:, u : u + e1 - e0, :].rearrange("p e x -> p (e x)"),
+            )
+
+        def weights(name, e, c0, c1):
+            if name == "q":
+                return wq_codes[:, e, PACK * c0 : PACK * c1].bitcast(FP8X4), wq_plane[:, e, c0:c1]
+            if name == "k":
+                return wk_codes[:, e, c0:c1].bitcast(FP8X4), wk_plane[:, e, c0:c1]
+            return wv_codes[:, e, 2 * c0 : 2 * c1].bitcast(FP4X4), wv_plane[:, e, c0:c1]
+
+        def grads(name, e, u0, u1):
+            e0 = first_of[e]
+            s0, s1 = (e - e0) * C + u0, (e - e0) * C + u1
+            return slot_words[name, e0][:, s0:s1].bitcast(FP8X4), slot_scales[name, e0][:, s0:s1]
+
+        def product(bank, stationary, moving, start, stop):
+            nc.tensor.matmul_mx(out=bank, lhsT=stationary[0], lhsT_scale=stationary[1],
+                                rhs=moving[0], rhs_scale=moving[1], start=start, stop=stop)
+
+        def expert_by_slots(e):
+            bank = acc_pool.tile([P, BLOCKS, K], F32, name="acc%d" % (e % ACC_BANKS))
+            passes = [("v", b, h * P, (h + 1) * P) for b in range(BLOCKS) for h in range(HALVES)]
+            passes += [(name, b, 0, K) for name in ("q", "k") for b in range(BLOCKS)]
+            for i, (name, b, c0, c1) in enumerate(passes):
+                product(bank[:, b, c0:c1], grads(name, e, b * P, (b + 1) * P), weights(name, e, c0, c1),
+                        i == 0, i == len(passes) - 1)
+            gated = ring.tile([P, BLOCKS, K], F32, name="gated")
+            for b in range(BLOCKS):
+                col = e * BLOCKS + b
+                nc.scalar.activation(gated[:, b, :], bank[:, b, :], COPY, scale=gate_cols[:, col : col + 1])
+            turned = turn_pool.tile([P, HALVES, C], F32, name="turn")
+            for h in range(HALVES):
+                for b in range(BLOCKS):
+                    nc.tensor.transpose(turned[:, h, b * P : (b + 1) * P], gated[:, b, h * P : (h + 1) * P], ident[:])
+            for h in range(HALVES):
+                nc.scalar.copy(dx[h][:, e * C : (e + 1) * C], turned[:, h, :])
+
+        def expert_by_features(e):
+            s0 = e * C
+            banks = [acc_pool.tile([P, C], F32, name="acc%d" % ((e - HALVES + h) % ACC_BANKS)) for h in range(HALVES)]
+            passes = [("v", b * P, (b + 1) * P) for b in range(BLOCKS)] + [("q", 0, C), ("k", 0, C)]
+            for i, (name, u0, u1) in enumerate(passes):
+                for h in range(HALVES):
+                    product(banks[h][:, u0:u1], weights(name, e, h * P, (h + 1) * P), grads(name, e, u0, u1),
+                            i == 0, i == len(passes) - 1)
+            for h in range(HALVES):
+                nc.vector.tensor_tensor(dx[h][:, s0 : s0 + C], banks[h][:], gate_last[:], MULT)
+
+        for e in range(E):
+            round_weights(e)
+
+        for e0, e1 in STRETCHES[:-1]:
+            gather_words("q", e0, e1, None)
+
+        for i, (e0, e1) in enumerate(STRETCHES):
+            before = i - 1 if i > 0 else None
+            if e0 == LAST:
+                gather_words("q", e0, e1, before)
+            gather_words("v", e0, e1, before)
+            gather_words("k", e0, e1, before)
+            gather_scales("v", e0, e1, before)
+            gather_scales("q", e0, e1, before)
+            if e0 % GROUP == 0:
+                quantize(e0, e0 + 2)
+                quantize(e0 + 2, e0 + 3)
+            gather_scales("k", e0, e1, e0 // GROUP)
+            for e in range(e0, e1):
+                if e == LAST:
+                    expert_by_features(e)
+                else:
+                    expert_by_slots(e)
+
+        picked = [[keep.tile([P, T], F32, name="picked%d_%d" % (h, r)) for r in range(TOP)] for h in range(HALVES)]
+        pair = [[keep.tile([P, T], F32, name="pair%d_%d" % (h, i)) for i in range(2)] for h in range(HALVES)]
+        total = [keep.tile([P, T], F32, name="total%d" % h) for h in range(HALVES)]
+
+        def fetch(h, r):
+            nc.vector.tensor_copy(picked[h][r][:], dx[h][:].indirect(pos_sb[r][:]))
+
+        def add_pair(h, i):
+            nc.vector.tensor_tensor(pair[h][i][:], picked[h][2 * i][:], picked[h][2 * i + 1][:], ADD)
+
+        def finish(h, t0, t1):
+            nc.vector.tensor_tensor(total[h][:, t0:t1], pair[h][0][:, t0:t1], pair[h][1][:, t0:t1], ADD)
+            nc.sync.dma_start(out[h * P : (h + 1) * P, t0:t1], total[h][:, t0:t1])
+
+        for r in range(TOP):
+            fetch(0, r)
+        fetch(1, 0)
+        add_pair(0, 0)
+        add_pair(0, 1)
+        fetch(1, 1)
+        finish(0, 0, T)
+        fetch(1, 2)
+        fetch(1, 3)
+        add_pair(1, 0)
+        add_pair(1, 1)
+        finish(1, 0, T // 2)
+        finish(1, T // 2, T)

@@ -29,6 +29,8 @@ STRETCHES = [(0, 3), (3, 6), (6, 9), (9, 11), (11, 12)]
 GROUP = 3
 RAW_BYTES = GROUP * PACK * K * 4
 ACC_BANKS = 4
+PIECES = 2
+PIECE = T // PIECES
 
 
 def tile_moe_qkb_kernel(
@@ -178,18 +180,18 @@ def tile_moe_qkb_kernel(
             for h in range(HALVES):
                 for b in range(BLOCKS):
                     nc.tensor.transpose(turned[:, h, b * P : (b + 1) * P], gated[:, b, h * P : (h + 1) * P], ident[:])
-            for h in range(HALVES):
+            for h in (1, 0):
                 nc.scalar.copy(dx[h][:, e * C : (e + 1) * C], turned[:, h, :])
 
         def expert_by_features(e):
             s0 = e * C
-            banks = [acc_pool.tile([P, C], F32, name="acc%d" % ((e - HALVES + h) % ACC_BANKS)) for h in range(HALVES)]
+            banks = [acc_pool.tile([P, C], F32, name="acc%d" % ((e - 1 - h) % ACC_BANKS)) for h in range(HALVES)]
             passes = [("v", b * P, (b + 1) * P) for b in range(BLOCKS)] + [("q", 0, C), ("k", 0, C)]
             for i, (name, u0, u1) in enumerate(passes):
-                for h in range(HALVES):
+                for h in (1, 0):
                     product(banks[h][:, u0:u1], weights(name, e, h * P, (h + 1) * P), grads(name, e, u0, u1),
                             i == 0, i == len(passes) - 1)
-            for h in range(HALVES):
+            for h in (1, 0):
                 nc.vector.tensor_tensor(dx[h][:, s0 : s0 + C], banks[h][:], gate_last[:], MULT)
 
         for e in range(E):
@@ -217,29 +219,50 @@ def tile_moe_qkb_kernel(
                     expert_by_slots(e)
 
         picked = [[keep.tile([P, T], F32, name="picked%d_%d" % (h, r)) for r in range(TOP)] for h in range(HALVES)]
-        pair = [[keep.tile([P, T], F32, name="pair%d_%d" % (h, i)) for i in range(2)] for h in range(HALVES)]
+        by_token = [keep.tile([P, T], F32, name="by_token%d" % h) for h in range(HALVES)]
         total = [keep.tile([P, T], F32, name="total%d" % h) for h in range(HALVES)]
 
-        def fetch(h, r):
-            nc.vector.tensor_copy(picked[h][r][:], dx[h][:].indirect(pos_sb[r][:]))
+        def fetch(h, r, t0, t1):
+            nc.vector.tensor_copy(picked[h][r][:, t0:t1], dx[h][:].indirect(pos_sb[r][:, t0 // 16 : t1 // 16]))
 
-        def add_pair(h, i):
-            nc.vector.tensor_tensor(pair[h][i][:], picked[h][2 * i][:], picked[h][2 * i + 1][:], ADD)
+        def add_turned(banks, h, r, first, last):
+            for i in range(PIECES):
+                for b in range(PIECE // P):
+                    t0 = i * PIECE + b * P
+                    nc.tensor.matmul(banks[i][:, b * P : (b + 1) * P], picked[h][r][:, t0 : t0 + P], ident[:],
+                                     start=(first and b == 0), stop=(last and b == PIECE // P - 1), is_transpose=True)
 
-        def finish(h, t0, t1):
-            nc.vector.tensor_tensor(total[h][:, t0:t1], pair[h][0][:, t0:t1], pair[h][1][:, t0:t1], ADD)
-            nc.sync.dma_start(out[h * P : (h + 1) * P, t0:t1], total[h][:, t0:t1])
+        def turn_back(banks, back, h, i):
+            nc.scalar.copy(by_token[h][:, i * PIECE : (i + 1) * PIECE], banks[i][:])
+            for b in range(PIECE // P):
+                t0 = i * PIECE + b * P
+                nc.tensor.transpose(back[:, b * P : (b + 1) * P], by_token[h][:, t0 : t0 + P], ident[:])
 
+        def store(h, i):
+            nc.sync.dma_start(out[h * P : (h + 1) * P, i * PIECE : (i + 1) * PIECE],
+                              total[h][:, i * PIECE : (i + 1) * PIECE])
+
+        sums1 = [acc_pool.tile([P, PIECE], F32, name="sum%d" % i) for i in range(PIECES)]
+        for r in range(TOP - 1):
+            fetch(1, r, 0, T)
+            add_turned(sums1, 1, r, r == 0, r == TOP - 2)
+        back1 = [acc_pool.tile([P, PIECE], F32, name="acc%d" % (1 + i)) for i in range(PIECES)]
+        for i in range(PIECES):
+            turn_back(sums1, back1[i], 1, i)
+
+        sums0 = [acc_pool.tile([P, PIECE], F32, name="acc%d" % (3 * i)) for i in range(PIECES)]
         for r in range(TOP):
-            fetch(0, r)
-        fetch(1, 0)
-        add_pair(0, 0)
-        add_pair(0, 1)
-        fetch(1, 1)
-        finish(0, 0, T)
-        fetch(1, 2)
-        fetch(1, 3)
-        add_pair(1, 0)
-        add_pair(1, 1)
-        finish(1, 0, T // 2)
-        finish(1, T // 2, T)
+            fetch(0, r, 0, T)
+            add_turned(sums0, 0, r, r == 0, r == TOP - 1)
+        for i in range(PIECES):
+            back0 = turn_pool.tile([P, PIECE], F32, name="turn")
+            turn_back(sums0, back0, 0, i)
+            nc.scalar.copy(total[0][:, i * PIECE : (i + 1) * PIECE], back0[:])
+            store(0, i)
+
+        for i in range(PIECES):
+            fetch(1, TOP - 1, i * PIECE, (i + 1) * PIECE)
+        for i in range(PIECES):
+            cols = slice(i * PIECE, (i + 1) * PIECE)
+            nc.vector.tensor_tensor(total[1][:, cols], back1[i][:], picked[1][TOP - 1][:, cols], ADD)
+            store(1, i)

@@ -25,10 +25,14 @@ WINDOW = 1024
 HALVES = K // P
 BLOCKS = C // P
 LAST = E - 1
-STRETCHES = [(0, 3), (3, 6), (6, 9), (9, 11), (11, 12)]
+STRETCHES = [(0, 3), (3, 6), (6, 9), (9, 10), (10, 11), (11, 12)]
+EARLY_Q = [(0, 3), (3, 6), (6, 9), (9, 11)]
+BANK = 512
+BANK_BYTES = 4 * BANK
 GROUP = 3
 RAW_BYTES = GROUP * PACK * K * 4
 ACC_BANKS = 4
+WQ_ROW = 4
 PIECES = 2
 PIECE = T // PIECES
 
@@ -42,15 +46,16 @@ def tile_moe_qkb_kernel(
         keep = ctx.enter_context(tc.tile_pool(name="keep", bufs=1))
         ring = ctx.enter_context(tc.tile_pool(name="ring", bufs=3))
         shared = ctx.enter_context(tc.tile_pool(name="shared", bufs=1))
-        acc_pool = ctx.enter_context(tc.psum_pool(name="acc", bufs=1))
-        turn_pool = ctx.enter_context(tc.psum_pool(name="turn", bufs=2))
+        psum = ctx.enter_context(tc.psum_pool(name="psum", bufs=1))
+
+        def banks_at(name, first, shape):
+            return psum.tile(shape, F32, name=name, offset=first * BANK_BYTES)
 
         offs_sb = keep.tile([P, SLOTS // 16], U16, name="offs_sb")
         pos_sb = [keep.tile([P, T // 16], U16, name="pos_sb%d" % r) for r in range(TOP)]
         nc.sync.dma_start(offs_sb[:], offs)
 
         tok_words, tok_scales, slot_words, slot_scales = {}, {}, {}, {}
-        first_of = {e: e0 for e0, e1 in STRETCHES for e in range(e0, e1)}
         for name, words in (("q", dq_words), ("v", dv_words), ("k", dk_words)):
             tok_words[name] = keep.tile([P, WINDOW], I32, name="tok_words_" + name, align_bytes=64)
             nc.vector.memset(tok_words[name][:, T:WINDOW], 0)
@@ -67,15 +72,13 @@ def tile_moe_qkb_kernel(
         wq_codes = keep.tile([P, E, K * PACK], U8, name="wq_codes", align_bytes=64)
         wv_codes = keep.tile([P, E, K * 2], U8, name="wv_codes", align_bytes=64)
         wk_codes = keep.tile([P, E, K], U32, name="wk_codes", align_bytes=64)
-        wq_plane = keep.tile([P, E, K], U8, name="wq_plane", align_bytes=64)
-        wv_plane = keep.tile([P, E, K], U8, name="wv_plane", align_bytes=64)
+        packed_planes = keep.tile([P, E, K], U8, name="packed_planes", align_bytes=64)
         wk_plane = keep.tile([P, E, K], U8, name="wk_plane", align_bytes=64)
         wk_raw = [shared.tile([P, GROUP, PACK, K], F32, name="wk_raw%d" % g, align_bytes=64, offset=g * RAW_BYTES)
                   for g in range(E // GROUP)]
         rounded = [keep.tile([P, GROUP, K * PACK], BF16, name="rounded%d" % g, align_bytes=64)
                    for g in range(E // GROUP)]
-        nc.vector.memset(wv_plane[:].bitcast(I32), 0)
-        nc.vector.memset(wq_plane[:].bitcast(I32), 0)
+        nc.vector.memset(packed_planes[:].bitcast(I32), 0)
 
         def load_wk(e):
             nc.sync.dma_start(wk_raw[e // GROUP][:, e % GROUP, :, :], wk[e].rearrange("(p j) c -> p j c", j=PACK))
@@ -90,16 +93,14 @@ def tile_moe_qkb_kernel(
         gate_cols = keep.tile([P, E * BLOCKS], F32, name="gate_cols")
         gate_last = keep.tile([P, C], F32, name="gate_last")
 
-        for e in range(0, 3):
+        for e in range(0, 6):
             load_wk(e)
-        for plane, scales in ((wv_plane, wv_scales), (wq_plane, wq_scales)):
+        for row, scales in ((0, wv_scales), (WQ_ROW, wq_scales)):
             for r in range(4):
-                nc.sync.dma_start(plane[r:P:32, :, :].bitcast(I32),
+                nc.sync.dma_start(packed_planes[row + r : P : 32, :, :].bitcast(I32),
                                   scales[:, 0, r:16:4, :].rearrange("e b c -> b e c").bitcast(I32))
         nc.sync.dma_start(gate_rows[:], gate.rearrange("r (b p) -> (r b) p", p=P)[0:P, :])
         load_packed(0, 3)
-        for e in range(3, 6):
-            load_wk(e)
         load_packed(3, 6)
         for e in range(6, 12):
             load_wk(e)
@@ -108,8 +109,8 @@ def tile_moe_qkb_kernel(
         for r, pos in enumerate((pos1, pos2, pos3, pos4)):
             nc.sync.dma_start(pos_sb[r][:], pos)
 
-        gate_bank = turn_pool.tile([P, 4 * P], F32, name="turn")
-        nc.tensor.transpose(gate_bank[:, 0:P], gate_rows[:], ident[:])
+        gate_bank = banks_at("gate_bank", 6, [P, P])
+        nc.tensor.transpose(gate_bank[:], gate_rows[:], ident[:])
         nc.scalar.copy(gate_cols[:], gate_bank[:, 0 : E * BLOCKS])
 
         dx = [keep.tile([P, SLOTS], F32, name="dx%d" % h) for h in range(HALVES)]
@@ -129,12 +130,16 @@ def tile_moe_qkb_kernel(
             nc.vector.tensor_copy(dst[:], window.indirect(offs_sb[:, e0 * C // 16 : e1 * C // 16]))
 
         def gather_words(name, e0, e1, after):
-            slot_words[name, e0] = slot_tile(U32, 4, "words_" + name, e0, e1, after)
-            gather(slot_words[name, e0], tok_words[name][:].bitcast(U32), e0, e1)
+            dst = slot_tile(U32, 4, "words_" + name, e0, e1, after)
+            gather(dst, tok_words[name][:].bitcast(U32), e0, e1)
+            for e in range(e0, e1):
+                slot_words[name, e] = dst[:, (e - e0) * C : (e - e0 + 1) * C]
 
         def gather_scales(name, e0, e1, after):
-            slot_scales[name, e0] = slot_tile(U8, 1, "scales_" + name, e0, e1, after)
-            gather(slot_scales[name, e0], tok_scales[name][:], e0, e1)
+            dst = slot_tile(U8, 1, "scales_" + name, e0, e1, after)
+            gather(dst, tok_scales[name][:], e0, e1)
+            for e in range(e0, e1):
+                slot_scales[name, e] = dst[:, (e - e0) * C : (e - e0 + 1) * C]
 
         def round_weights(e):
             g, u = divmod(e, GROUP)
@@ -151,22 +156,20 @@ def tile_moe_qkb_kernel(
 
         def weights(name, e, c0, c1):
             if name == "q":
-                return wq_codes[:, e, PACK * c0 : PACK * c1].bitcast(FP8X4), wq_plane[:, e, c0:c1]
+                return wq_codes[:, e, PACK * c0 : PACK * c1].bitcast(FP8X4), packed_planes[WQ_ROW:P, e, c0:c1]
             if name == "k":
                 return wk_codes[:, e, c0:c1].bitcast(FP8X4), wk_plane[:, e, c0:c1]
-            return wv_codes[:, e, 2 * c0 : 2 * c1].bitcast(FP4X4), wv_plane[:, e, c0:c1]
+            return wv_codes[:, e, 2 * c0 : 2 * c1].bitcast(FP4X4), packed_planes[:, e, c0:c1]
 
         def grads(name, e, u0, u1):
-            e0 = first_of[e]
-            s0, s1 = (e - e0) * C + u0, (e - e0) * C + u1
-            return slot_words[name, e0][:, s0:s1].bitcast(FP8X4), slot_scales[name, e0][:, s0:s1]
+            return slot_words[name, e][:, u0:u1].bitcast(FP8X4), slot_scales[name, e][:, u0:u1]
 
         def product(bank, stationary, moving, start, stop):
             nc.tensor.matmul_mx(out=bank, lhsT=stationary[0], lhsT_scale=stationary[1],
                                 rhs=moving[0], rhs_scale=moving[1], start=start, stop=stop)
 
         def expert_by_slots(e):
-            bank = acc_pool.tile([P, BLOCKS, K], F32, name="acc%d" % (e % ACC_BANKS))
+            bank = banks_at("acc%d" % (e % ACC_BANKS), e % ACC_BANKS, [P, BLOCKS, K])
             passes = [("v", b, h * P, (h + 1) * P) for b in range(BLOCKS) for h in range(HALVES)]
             passes += [(name, b, 0, K) for name in ("q", "k") for b in range(BLOCKS)]
             for i, (name, b, c0, c1) in enumerate(passes):
@@ -176,7 +179,7 @@ def tile_moe_qkb_kernel(
             for b in range(BLOCKS):
                 col = e * BLOCKS + b
                 nc.scalar.activation(gated[:, b, :], bank[:, b, :], COPY, scale=gate_cols[:, col : col + 1])
-            turned = turn_pool.tile([P, HALVES, C], F32, name="turn")
+            turned = banks_at("turn%d" % (e % 2), ACC_BANKS + e % 2, [P, HALVES, C])
             for h in range(HALVES):
                 for b in range(BLOCKS):
                     nc.tensor.transpose(turned[:, h, b * P : (b + 1) * P], gated[:, b, h * P : (h + 1) * P], ident[:])
@@ -185,23 +188,23 @@ def tile_moe_qkb_kernel(
 
         def expert_by_features(e):
             s0 = e * C
-            banks = [acc_pool.tile([P, C], F32, name="acc%d" % ((e - 1 - h) % ACC_BANKS)) for h in range(HALVES)]
+            banks = banks_at("last", (e - 1) % ACC_BANKS, [P, HALVES, BANK])
             passes = [("v", b * P, (b + 1) * P) for b in range(BLOCKS)] + [("q", 0, C), ("k", 0, C)]
             for i, (name, u0, u1) in enumerate(passes):
                 for h in (1, 0):
-                    product(banks[h][:, u0:u1], weights(name, e, h * P, (h + 1) * P), grads(name, e, u0, u1),
+                    product(banks[:, h, u0:u1], weights(name, e, h * P, (h + 1) * P), grads(name, e, u0, u1),
                             i == 0, i == len(passes) - 1)
             for h in (1, 0):
-                nc.vector.tensor_tensor(dx[h][:, s0 : s0 + C], banks[h][:], gate_last[:], MULT)
+                nc.vector.tensor_tensor(dx[h][:, s0 : s0 + C], banks[:, h, 0:C], gate_last[:], MULT)
 
         for e in range(E):
             round_weights(e)
 
-        for e0, e1 in STRETCHES[:-1]:
+        for e0, e1 in EARLY_Q:
             gather_words("q", e0, e1, None)
 
-        for i, (e0, e1) in enumerate(STRETCHES):
-            before = i - 1 if i > 0 else None
+        for e0, e1 in STRETCHES:
+            before = (e0 - 1) // GROUP if e0 > 0 else None
             if e0 == LAST:
                 gather_words("q", e0, e1, before)
             gather_words("v", e0, e1, before)
@@ -242,27 +245,20 @@ def tile_moe_qkb_kernel(
             nc.sync.dma_start(out[h * P : (h + 1) * P, i * PIECE : (i + 1) * PIECE],
                               total[h][:, i * PIECE : (i + 1) * PIECE])
 
-        sums1 = [acc_pool.tile([P, PIECE], F32, name="sum%d" % i) for i in range(PIECES)]
-        for r in range(TOP - 1):
-            fetch(1, r, 0, T)
-            add_turned(sums1, 1, r, r == 0, r == TOP - 2)
-        back1 = [acc_pool.tile([P, PIECE], F32, name="acc%d" % (1 + i)) for i in range(PIECES)]
-        for i in range(PIECES):
-            turn_back(sums1, back1[i], 1, i)
+        back = {}
+        for h, sum_bank, back_bank in ((1, 6, 0), (0, 4, 2)):
+            sums = [banks_at("sum%d_%d" % (h, i), sum_bank + i, [P, PIECE]) for i in range(PIECES)]
+            for r in range(TOP - 1):
+                fetch(h, r, 0, T)
+                add_turned(sums, h, r, r == 0, r == TOP - 2)
+            for i in range(PIECES):
+                back[h, i] = banks_at("back%d_%d" % (h, i), back_bank + i, [P, PIECE])
+                turn_back(sums, back[h, i], h, i)
 
-        sums0 = [acc_pool.tile([P, PIECE], F32, name="acc%d" % (3 * i)) for i in range(PIECES)]
-        for r in range(TOP):
-            fetch(0, r, 0, T)
-            add_turned(sums0, 0, r, r == 0, r == TOP - 1)
-        for i in range(PIECES):
-            back0 = turn_pool.tile([P, PIECE], F32, name="turn")
-            turn_back(sums0, back0, 0, i)
-            nc.scalar.copy(total[0][:, i * PIECE : (i + 1) * PIECE], back0[:])
-            store(0, i)
-
-        for i in range(PIECES):
-            fetch(1, TOP - 1, i * PIECE, (i + 1) * PIECE)
-        for i in range(PIECES):
-            cols = slice(i * PIECE, (i + 1) * PIECE)
-            nc.vector.tensor_tensor(total[1][:, cols], back1[i][:], picked[1][TOP - 1][:, cols], ADD)
-            store(1, i)
+        for h in (1, 0):
+            for i in range(PIECES):
+                fetch(h, TOP - 1, i * PIECE, (i + 1) * PIECE)
+            for i in range(PIECES):
+                cols = slice(i * PIECE, (i + 1) * PIECE)
+                nc.vector.tensor_tensor(total[h][:, cols], back[h, i][:], picked[h][TOP - 1][:, cols], ADD)
+                store(h, i)

@@ -126,8 +126,12 @@ def tile_moe_qkb_kernel(
             assert used[after] <= RAW_BYTES
             return shared.tile(shape, dtype, name=name, align_bytes=64, offset=offset)
 
-        def gather(dst, window, e0, e1):
-            nc.vector.tensor_copy(dst[:], window.indirect(offs_sb[:, e0 * C // 16 : e1 * C // 16]))
+        def gather(dst, window, e0, e1, cuts=1):
+            width = (e1 - e0) * C // cuts
+            for i in range(cuts):
+                s0 = e0 * C + i * width
+                nc.vector.tensor_copy(dst[:, i * width : (i + 1) * width],
+                                      window.indirect(offs_sb[:, s0 // 16 : (s0 + width) // 16]))
 
         def gather_words(name, e0, e1, after):
             dst = slot_tile(U32, 4, "words_" + name, e0, e1, after)
@@ -135,9 +139,9 @@ def tile_moe_qkb_kernel(
             for e in range(e0, e1):
                 slot_words[name, e] = dst[:, (e - e0) * C : (e - e0 + 1) * C]
 
-        def gather_scales(name, e0, e1, after):
+        def gather_scales(name, e0, e1, after, cuts=1):
             dst = slot_tile(U8, 1, "scales_" + name, e0, e1, after)
-            gather(dst, tok_scales[name][:], e0, e1)
+            gather(dst, tok_scales[name][:], e0, e1, cuts)
             for e in range(e0, e1):
                 slot_scales[name, e] = dst[:, (e - e0) * C : (e - e0 + 1) * C]
 
@@ -183,19 +187,21 @@ def tile_moe_qkb_kernel(
             for h in range(HALVES):
                 for b in range(BLOCKS):
                     nc.tensor.transpose(turned[:, h, b * P : (b + 1) * P], gated[:, b, h * P : (h + 1) * P], ident[:])
-            for h in (1, 0):
+            for h in range(HALVES):
                 nc.scalar.copy(dx[h][:, e * C : (e + 1) * C], turned[:, h, :])
 
         def expert_by_features(e):
-            s0 = e * C
-            banks = banks_at("last", (e - 1) % ACC_BANKS, [P, HALVES, BANK])
-            passes = [("v", b * P, (b + 1) * P) for b in range(BLOCKS)] + [("q", 0, C), ("k", 0, C)]
-            for i, (name, u0, u1) in enumerate(passes):
-                for h in (1, 0):
-                    product(banks[:, h, u0:u1], weights(name, e, h * P, (h + 1) * P), grads(name, e, u0, u1),
-                            i == 0, i == len(passes) - 1)
-            for h in (1, 0):
-                nc.vector.tensor_tensor(dx[h][:, s0 : s0 + C], banks[:, h, 0:C], gate_last[:], MULT)
+            banks = banks_at("last", (e - 1) % ACC_BANKS, [P, BLOCKS, BANK])
+            for name in ("v", "q", "k"):
+                for b in range(BLOCKS):
+                    for h in range(HALVES):
+                        product(banks[:, b, h * P : (h + 1) * P], weights(name, e, h * P, (h + 1) * P),
+                                grads(name, e, b * P, (b + 1) * P), name == "v" and h == 0, name == "k" and h == HALVES - 1)
+            for b in range(BLOCKS):
+                for h in range(HALVES):
+                    s0 = e * C + b * P
+                    nc.vector.tensor_tensor(dx[h][:, s0 : s0 + P], banks[:, b, h * P : (h + 1) * P],
+                                            gate_last[:, b * P : (b + 1) * P], MULT)
 
         for e in range(E):
             round_weights(e)
@@ -214,7 +220,7 @@ def tile_moe_qkb_kernel(
             if e0 % GROUP == 0:
                 quantize(e0, e0 + 2)
                 quantize(e0 + 2, e0 + 3)
-            gather_scales("k", e0, e1, e0 // GROUP)
+            gather_scales("k", e0, e1, e0 // GROUP, BLOCKS if e0 == LAST else 1)
             for e in range(e0, e1):
                 if e == LAST:
                     expert_by_features(e)
@@ -228,37 +234,49 @@ def tile_moe_qkb_kernel(
         def fetch(h, r, t0, t1):
             nc.vector.tensor_copy(picked[h][r][:, t0:t1], dx[h][:].indirect(pos_sb[r][:, t0 // 16 : t1 // 16]))
 
-        def add_turned(banks, h, r, first, last):
-            for i in range(PIECES):
-                for b in range(PIECE // P):
-                    t0 = i * PIECE + b * P
-                    nc.tensor.matmul(banks[i][:, b * P : (b + 1) * P], picked[h][r][:, t0 : t0 + P], ident[:],
-                                     start=(first and b == 0), stop=(last and b == PIECE // P - 1), is_transpose=True)
+        def add_turned(bank, h, r, i, first, last):
+            for b in range(PIECE // P):
+                t0 = i * PIECE + b * P
+                nc.tensor.matmul(bank[:, b * P : (b + 1) * P], picked[h][r][:, t0 : t0 + P], ident[:],
+                                 start=(first and b == 0), stop=(last and b == PIECE // P - 1), is_transpose=True)
 
-        def turn_back(banks, back, h, i):
-            nc.scalar.copy(by_token[h][:, i * PIECE : (i + 1) * PIECE], banks[i][:])
+        def turn_back(bank, h, i, back_bank):
+            nc.scalar.copy(by_token[h][:, i * PIECE : (i + 1) * PIECE], bank[:])
+            back = banks_at("back%d_%d" % (h, i), back_bank, [P, PIECE])
             for b in range(PIECE // P):
                 t0 = i * PIECE + b * P
                 nc.tensor.transpose(back[:, b * P : (b + 1) * P], by_token[h][:, t0 : t0 + P], ident[:])
+            return back
 
-        def store(h, i):
-            nc.sync.dma_start(out[h * P : (h + 1) * P, i * PIECE : (i + 1) * PIECE],
-                              total[h][:, i * PIECE : (i + 1) * PIECE])
+        def store(h, t0, t1):
+            nc.sync.dma_start(out[h * P : (h + 1) * P, t0:t1], total[h][:, t0:t1])
 
-        back = {}
-        for h, sum_bank, back_bank in ((1, 6, 0), (0, 4, 2)):
-            sums = [banks_at("sum%d_%d" % (h, i), sum_bank + i, [P, PIECE]) for i in range(PIECES)]
-            for r in range(TOP - 1):
-                fetch(h, r, 0, T)
-                add_turned(sums, h, r, r == 0, r == TOP - 2)
-            for i in range(PIECES):
-                back[h, i] = banks_at("back%d_%d" % (h, i), back_bank + i, [P, PIECE])
-                turn_back(sums, back[h, i], h, i)
+        def finish(back, h, i, u0, u1):
+            t0, t1 = i * PIECE + u0, i * PIECE + u1
+            nc.vector.tensor_tensor(total[h][:, t0:t1], back[:, u0:u1], picked[h][TOP - 1][:, t0:t1], ADD)
+            store(h, t0, t1)
 
-        for h in (1, 0):
+        sums0 = [banks_at("sum0_%d" % i, 6 + i, [P, PIECE]) for i in range(PIECES)]
+        for r in range(TOP):
+            fetch(0, r, 0, T)
             for i in range(PIECES):
-                fetch(h, TOP - 1, i * PIECE, (i + 1) * PIECE)
+                add_turned(sums0[i], 0, r, i, r == 0, r == TOP - 1)
+        for i in range(PIECES):
+            back0 = turn_back(sums0[i], 0, i, i)
+            nc.scalar.copy(total[0][:, i * PIECE : (i + 1) * PIECE], back0[:])
+            store(0, i * PIECE, (i + 1) * PIECE)
+
+        sums1 = [banks_at("sum1_%d" % i, 4 + i, [P, PIECE]) for i in range(PIECES)]
+        for r in range(TOP - 2):
+            fetch(1, r, 0, T)
             for i in range(PIECES):
-                cols = slice(i * PIECE, (i + 1) * PIECE)
-                nc.vector.tensor_tensor(total[h][:, cols], back[h, i][:], picked[h][TOP - 1][:, cols], ADD)
-                store(h, i)
+                add_turned(sums1[i], 1, r, i, r == 0, False)
+        back1 = []
+        for i in range(PIECES):
+            fetch(1, TOP - 2, i * PIECE, (i + 1) * PIECE)
+            add_turned(sums1[i], 1, TOP - 2, i, False, True)
+            back1.append(turn_back(sums1[i], 1, i, 2 + i))
+        for i in range(PIECES):
+            fetch(1, TOP - 1, i * PIECE, (i + 1) * PIECE)
+        for i in range(PIECES):
+            finish(back1[i], 1, i, 0, PIECE)

from contextlib import ExitStack

import concourse.mybir as mybir
from concourse.masks import make_identity

K, T, E, C, N, TOP = 256, 768, 12, 256, 512, 4
SLOTS = E * C
FLOPS = 2 * 3 * SLOTS * N * K

F32 = mybir.dt.float32
BF16 = mybir.dt.bfloat16
I32 = mybir.dt.int32
U32 = mybir.dt.uint32
U16 = mybir.dt.uint16
U8 = mybir.dt.uint8
FP8X4 = mybir.dt.float8_e4m3fn_x4
FP4X4 = mybir.dt.float4_e2m1fn_x4
MULT = mybir.AluOpType.mult
ADD = mybir.AluOpType.add
COPY = mybir.ActivationFunctionType.Copy

P = 128
PACK = 4
WINDOW = 1024
HALVES = K // P
BLOCKS = C // P
LAST = E - 1
STRETCHES = [(0, 3), (3, 6), (6, 9), (9, 10), (10, 11), (11, 12)]
EARLY_Q = [(0, 3), (3, 6), (6, 9), (9, 11)]
BANK = 512
BANK_BYTES = 4 * BANK
GROUP = 3
RAW_BYTES = GROUP * PACK * K * 4
ACC_BANKS = 4
WQ_ROW = 4
PIECES = 2
PIECE = T // PIECES


def tile_moe_qkb_kernel(
    tc, dq_words, dq_scales, dk_words, dk_scales, dv_words, dv_scales, wq_words, wq_scales, wk,
    wv_words, wv_scales, gate, offs, pos1, pos2, pos3, pos4, out,
):
    nc = tc.nc
    with ExitStack() as ctx:
        keep = ctx.enter_context(tc.tile_pool(name="keep", bufs=1))
        ring = ctx.enter_context(tc.tile_pool(name="ring", bufs=3))
        shared = ctx.enter_context(tc.tile_pool(name="shared", bufs=1))
        psum = ctx.enter_context(tc.psum_pool(name="psum", bufs=1))

        def banks_at(name, first, shape):
            return psum.tile(shape, F32, name=name, offset=first * BANK_BYTES)

        offs_sb = keep.tile([P, SLOTS // 16], U16, name="offs_sb")
        pos_sb = [keep.tile([P, T // 16], U16, name="pos_sb%d" % r) for r in range(TOP)]
        nc.sync.dma_start(offs_sb[:], offs)

        tok_words, tok_scales, slot_words, slot_scales = {}, {}, {}, {}
        for name, words in (("q", dq_words), ("v", dv_words), ("k", dk_words)):
            tok_words[name] = keep.tile([P, WINDOW], I32, name="tok_words_" + name, align_bytes=64)
            nc.vector.memset(tok_words[name][:, T:WINDOW], 0)
            nc.sync.dma_start(tok_words[name][:, 0:T], words[0].rearrange("p t d -> p (t d)").bitcast(I32))
        for name, scales in (("v", dv_scales), ("q", dq_scales), ("k", dk_scales)):
            tok_scales[name] = keep.tile([P, WINDOW], U8, name="tok_scales_" + name, align_bytes=64)
            nc.vector.memset(tok_scales[name][:].bitcast(I32), 0)
            for r in range(4):
                nc.sync.dma_start(tok_scales[name][r:P:32, 0:T].bitcast(I32), scales[0, r:16:4, :].bitcast(I32))

        ident = keep.tile([P, P], F32, name="ident")
        make_identity(nc, ident[:])

        wq_codes = keep.tile([P, E, K * PACK], U8, name="wq_codes", align_bytes=64)
        wv_codes = keep.tile([P, E, K * 2], U8, name="wv_codes", align_bytes=64)
        wk_codes = keep.tile([P, E, K], U32, name="wk_codes", align_bytes=64)
        packed_planes = keep.tile([P, E, K], U8, name="packed_planes", align_bytes=64)
        wk_plane = keep.tile([P, E, K], U8, name="wk_plane", align_bytes=64)
        wk_raw = [shared.tile([P, GROUP, PACK, K], F32, name="wk_raw%d" % g, align_bytes=64, offset=g * RAW_BYTES)
                  for g in range(E // GROUP)]
        rounded = [keep.tile([P, GROUP, K * PACK], BF16, name="rounded%d" % g, align_bytes=64)
                   for g in range(E // GROUP)]
        nc.vector.memset(packed_planes[:].bitcast(I32), 0)

        def load_wk(e):
            nc.sync.dma_start(wk_raw[e // GROUP][:, e % GROUP, :, :], wk[e].rearrange("(p j) c -> p j c", j=PACK))

        def load_packed(e0, e1):
            nc.sync.dma_start(wv_codes[:, e0:e1, :].bitcast(I32),
                              wv_words[e0:e1].rearrange("e s p b -> p (e s) b").bitcast(I32))
            nc.sync.dma_start(wq_codes[:, e0:e1, :].bitcast(I32),
                              wq_words[e0:e1].rearrange("e s p c d -> p (e s) (c d)").bitcast(I32))

        gate_rows = keep.tile([P, P], F32, name="gate_rows")
        gate_cols = keep.tile([P, E * BLOCKS], F32, name="gate_cols")
        gate_last = keep.tile([P, C], F32, name="gate_last")

        for e in range(0, 6):
            load_wk(e)
        for row, scales in ((0, wv_scales), (WQ_ROW, wq_scales)):
            for r in range(4):
                nc.sync.dma_start(packed_planes[row + r : P : 32, :, :].bitcast(I32),
                                  scales[:, 0, r:16:4, :].rearrange("e b c -> b e c").bitcast(I32))
        nc.sync.dma_start(gate_rows[:], gate.rearrange("r (b p) -> (r b) p", p=P)[0:P, :])
        load_packed(0, 3)
        load_packed(3, 6)
        for e in range(6, 12):
            load_wk(e)
        load_packed(6, 12)
        nc.sync.dma_start(gate_last[:], gate[:, LAST * C : SLOTS])
        for r, pos in enumerate((pos1, pos2, pos3, pos4)):
            nc.sync.dma_start(pos_sb[r][:], pos)

        gate_bank = banks_at("gate_bank", 6, [P, P])
        nc.tensor.transpose(gate_bank[:], gate_rows[:], ident[:])
        nc.scalar.copy(gate_cols[:], gate_bank[:, 0 : E * BLOCKS])

        dx = [keep.tile([P, SLOTS], F32, name="dx%d" % h) for h in range(HALVES)]

        used = [0] * (E // GROUP)

        def slot_tile(dtype, size, sort, e0, e1, after):
            shape, name = [P, (e1 - e0) * C], "%s_%d" % (sort, e0)
            if after is None:
                return keep.tile(shape, dtype, name=name, align_bytes=64)
            offset = after * RAW_BYTES + used[after]
            used[after] += shape[1] * size
            assert used[after] <= RAW_BYTES
            return shared.tile(shape, dtype, name=name, align_bytes=64, offset=offset)

        def gather(dst, window, e0, e1, cuts=1):
            width = (e1 - e0) * C // cuts
            for i in range(cuts):
                s0 = e0 * C + i * width
                nc.vector.tensor_copy(dst[:, i * width : (i + 1) * width],
                                      window.indirect(offs_sb[:, s0 // 16 : (s0 + width) // 16]))

        def gather_words(name, e0, e1, after):
            dst = slot_tile(U32, 4, "words_" + name, e0, e1, after)
            gather(dst, tok_words[name][:].bitcast(U32), e0, e1)
            for e in range(e0, e1):
                slot_words[name, e] = dst[:, (e - e0) * C : (e - e0 + 1) * C]

        def gather_scales(name, e0, e1, after, cuts=1):
            dst = slot_tile(U8, 1, "scales_" + name, e0, e1, after)
            gather(dst, tok_scales[name][:], e0, e1, cuts)
            for e in range(e0, e1):
                slot_scales[name, e] = dst[:, (e - e0) * C : (e - e0 + 1) * C]

        def round_weights(e):
            g, u = divmod(e, GROUP)
            nc.scalar.copy(rounded[g][:, u, :].rearrange("p (g i j) -> p g j i", i=4, j=PACK),
                           wk_raw[g][:, u, :, :].rearrange("p j (g i) -> p g j i", i=4))

        def quantize(e0, e1):
            g, u = divmod(e0, GROUP)
            nc.vector.quantize_mx(
                out=wk_codes[:, e0:e1, :].rearrange("p e c -> p (e c)").bitcast(FP8X4),
                scales=wk_plane[:, e0:e1, :].rearrange("p e c -> p (e c)"),
                in_=rounded[g][:, u : u + e1 - e0, :].rearrange("p e x -> p (e x)"),
            )

        def weights(name, e, c0, c1):
            if name == "q":
                return wq_codes[:, e, PACK * c0 : PACK * c1].bitcast(FP8X4), packed_planes[WQ_ROW:P, e, c0:c1]
            if name == "k":
                return wk_codes[:, e, c0:c1].bitcast(FP8X4), wk_plane[:, e, c0:c1]
            return wv_codes[:, e, 2 * c0 : 2 * c1].bitcast(FP4X4), packed_planes[:, e, c0:c1]

        def grads(name, e, u0, u1):
            return slot_words[name, e][:, u0:u1].bitcast(FP8X4), slot_scales[name, e][:, u0:u1]

        def product(bank, stationary, moving, start, stop):
            nc.tensor.matmul_mx(out=bank, lhsT=stationary[0], lhsT_scale=stationary[1],
                                rhs=moving[0], rhs_scale=moving[1], start=start, stop=stop)

        def expert_by_slots(e):
            bank = banks_at("acc%d" % (e % ACC_BANKS), e % ACC_BANKS, [P, BLOCKS, K])
            passes = [("v", b, h * P, (h + 1) * P) for b in range(BLOCKS) for h in range(HALVES)]
            passes += [(name, b, 0, K) for name in ("q", "k") for b in range(BLOCKS)]
            for i, (name, b, c0, c1) in enumerate(passes):
                product(bank[:, b, c0:c1], grads(name, e, b * P, (b + 1) * P), weights(name, e, c0, c1),
                        i == 0, i == len(passes) - 1)
            gated = ring.tile([P, BLOCKS, K], F32, name="gated")
            for b in range(BLOCKS):
                col = e * BLOCKS + b
                nc.scalar.activation(gated[:, b, :], bank[:, b, :], COPY, scale=gate_cols[:, col : col + 1])
            turned = banks_at("turn%d" % (e % 2), ACC_BANKS + e % 2, [P, HALVES, C])
            for h in range(HALVES):
                for b in range(BLOCKS):
                    nc.tensor.transpose(turned[:, h, b * P : (b + 1) * P], gated[:, b, h * P : (h + 1) * P], ident[:])
            for h in range(HALVES):
                nc.scalar.copy(dx[h][:, e * C : (e + 1) * C], turned[:, h, :])

        def expert_by_features(e):
            banks = banks_at("last", (e - 1) % ACC_BANKS, [P, BLOCKS, BANK])
            for name in ("v", "q", "k"):
                for b in range(BLOCKS):
                    for h in range(HALVES):
                        product(banks[:, b, h * P : (h + 1) * P], weights(name, e, h * P, (h + 1) * P),
                                grads(name, e, b * P, (b + 1) * P), name == "v" and h == 0, name == "k" and h == HALVES - 1)
            for b in range(BLOCKS):
                for h in range(HALVES):
                    s0 = e * C + b * P
                    nc.vector.tensor_tensor(dx[h][:, s0 : s0 + P], banks[:, b, h * P : (h + 1) * P],
                                            gate_last[:, b * P : (b + 1) * P], MULT)

        for e in range(E):
            round_weights(e)

        for e0, e1 in EARLY_Q:
            gather_words("q", e0, e1, None)

        for e0, e1 in STRETCHES:
            before = (e0 - 1) // GROUP if e0 > 0 else None
            if e0 == LAST:
                gather_words("q", e0, e1, before)
            gather_words("v", e0, e1, before)
            gather_words("k", e0, e1, before)
            gather_scales("v", e0, e1, before)
            gather_scales("q", e0, e1, before)
            if e0 % GROUP == 0:
                quantize(e0, e0 + 2)
                quantize(e0 + 2, e0 + 3)
            gather_scales("k", e0, e1, e0 // GROUP, BLOCKS if e0 == LAST else 1)
            for e in range(e0, e1):
                if e == LAST:
                    expert_by_features(e)
                else:
                    expert_by_slots(e)

        picked = [[keep.tile([P, T], F32, name="picked%d_%d" % (h, r)) for r in range(TOP)] for h in range(HALVES)]
        by_token = [keep.tile([P, T], F32, name="by_token%d" % h) for h in range(HALVES)]
        total = [keep.tile([P, T], F32, name="total%d" % h) for h in range(HALVES)]

        def fetch(h, r, t0, t1):
            nc.vector.tensor_copy(picked[h][r][:, t0:t1], dx[h][:].indirect(pos_sb[r][:, t0 // 16 : t1 // 16]))

        def add_turned(bank, h, r, i, first, last):
            for b in range(PIECE // P):
                t0 = i * PIECE + b * P
                nc.tensor.matmul(bank[:, b * P : (b + 1) * P], picked[h][r][:, t0 : t0 + P], ident[:],
                                 start=(first and b == 0), stop=(last and b == PIECE // P - 1), is_transpose=True)

        def turn_back(bank, h, i, back_bank):
            nc.scalar.copy(by_token[h][:, i * PIECE : (i + 1) * PIECE], bank[:])
            back = banks_at("back%d_%d" % (h, i), back_bank, [P, PIECE])
            for b in range(PIECE // P):
                t0 = i * PIECE + b * P
                nc.tensor.transpose(back[:, b * P : (b + 1) * P], by_token[h][:, t0 : t0 + P], ident[:])
            return back

        def store(h, t0, t1):
            nc.sync.dma_start(out[h * P : (h + 1) * P, t0:t1], total[h][:, t0:t1])

        def finish(back, h, i, u0, u1):
            t0, t1 = i * PIECE + u0, i * PIECE + u1
            nc.vector.tensor_tensor(total[h][:, t0:t1], back[:, u0:u1], picked[h][TOP - 1][:, t0:t1], ADD)
            store(h, t0, t1)

        sums0 = [banks_at("sum0_%d" % i, 6 + i, [P, PIECE]) for i in range(PIECES)]
        for r in range(TOP):
            fetch(0, r, 0, T)
            for i in range(PIECES):
                add_turned(sums0[i], 0, r, i, r == 0, r == TOP - 1)
        for i in range(PIECES):
            back0 = turn_back(sums0[i], 0, i, i)
            nc.scalar.copy(total[0][:, i * PIECE : (i + 1) * PIECE], back0[:])
            store(0, i * PIECE, (i + 1) * PIECE)

        sums1 = [banks_at("sum1_%d" % i, 4 + i, [P, PIECE]) for i in range(PIECES)]
        for r in range(TOP - 2):
            fetch(1, r, 0, T)
            for i in range(PIECES):
                add_turned(sums1[i], 1, r, i, r == 0, False)
        back1 = []
        for i in range(PIECES):
            fetch(1, TOP - 2, i * PIECE, (i + 1) * PIECE)
            add_turned(sums1[i], 1, TOP - 2, i, False, True)
            back1.append(turn_back(sums1[i], 1, i, 2 + i))
        for i in range(PIECES):
            fetch(1, TOP - 1, i * PIECE, (i + 1) * PIECE)
        for i in range(PIECES):
            finish(back1[i], 1, i, 0, PIECE)
